import numpy as np
import ml_dtypes

BF16 = ml_dtypes.bfloat16


def bf(x):
    return np.asarray(x, np.float32).astype(BF16)


def f32(x):
    return np.asarray(x, np.float32)


def f64(x):
    return np.asarray(x).astype(np.float64)


def striped(idx):
    return np.tile(idx.reshape(-1, 16).T, (8, 1))


S, K, M, N, V, D = 2048, 512, 128, 1024, 64, 16


def gelu_tanh(v):
    return 0.5 * v * (1.0 + np.tanh(np.sqrt(2.0 / np.pi) * (v + 0.044715 * v**3)))


def setup_inputs():
    return {"table": bf(np.random.standard_normal((K, S))), "w": bf(np.random.standard_normal((K, M)) / np.sqrt(K)), "c": f32((0.2 + 0.8 * np.random.random_sample((1, N))) / np.sqrt(D)), "b": f32(0.5 * np.random.standard_normal((M, 1))), "offs": striped(np.random.permutation(S)[:N])}


def reference(table, w, c, b, offs):
    idx = offs[:16].T.reshape(-1)
    y = (f64(w).T @ f64(table)[:, idx]).reshape(M, V, D)
    a = f64(c).reshape(V, D)
    z = (y * a).sum(axis=2)
    return gelu_tanh(z + f64(b))

@@ -1,0 +1,61 @@
+import concourse.mybir as mybir
+
+P = 128
+S, K, M, N = 2048, 512, 128, 1024
+BAG = 16
+BAGS = N // BAG
+BLOCKS = K // P
+PIECE = 512
+PIECES = N // PIECE
+LIST_ROWS = 16
+
+FLOPS = 2 * K * M * N + 2 * M * N
+
+BF16, F32, U16 = mybir.dt.bfloat16, mybir.dt.float32, mybir.dt.uint16
+ALU = mybir.AluOpType
+GELU = mybir.ActivationFunctionType.Gelu_apprx_tanh
+
+
+def tile_rows_wbag_gelu_sub_kernel(tc, table, w, c, b, offs, out):
+    nc = tc.nc
+    with (
+        tc.tile_pool(name="sbuf", bufs=1) as sbuf,
+        tc.psum_pool(name="psum", bufs=1) as psum,
+    ):
+        table_blocks = table.rearrange("(p a) s -> a p s", a=BLOCKS)
+        weights = sbuf.tile([P, BLOCKS, M], BF16)
+        offsets = sbuf.tile([P, N // LIST_ROWS], U16)
+        bias = sbuf.tile([P, 1], F32)
+        entry_weights = sbuf.tile([P, N], F32)
+        words = [sbuf.tile([P, S], BF16, name=f"words{a}") for a in range(BLOCKS)]
+
+        nc.sync.dma_start(offsets[:], offs)
+        nc.scalar.dma_start(weights[:], w.rearrange("(p a) m -> p a m", a=BLOCKS))
+        for a in range(BLOCKS):
+            nc.sync.dma_start(words[a][:], table_blocks[a])
+        nc.sync.dma_start(entry_weights[:], c[0].partition_broadcast(P))
+        nc.scalar.dma_start(bias[:], b)
+
+        projected = [psum.tile([P, PIECE], F32, name=f"projected{i}") for i in range(PIECES)]
+        columns = PIECE // LIST_ROWS
+        for a in range(BLOCKS):
+            for i in range(PIECES):
+                picked = words[a][:].indirect(offsets[:, i * columns : (i + 1) * columns])
+                nc.tensor.matmul(projected[i][:], weights[:, a, :], picked, start=a == 0, stop=a == BLOCKS - 1)
+
+        weighted = sbuf.tile([P, N], F32)
+        bag_sums = sbuf.tile([P, BAGS], F32)
+        for i in range(PIECES):
+            entries = slice(i * PIECE, (i + 1) * PIECE)
+            bags = slice(i * PIECE // BAG, (i + 1) * PIECE // BAG)
+            nc.vector.tensor_tensor(weighted[:, entries], projected[i][:], entry_weights[:, entries], ALU.mult)
+            nc.vector.tensor_reduce(
+                bag_sums[:, bags],
+                weighted[:, entries].rearrange("p (v t) -> p v t", t=BAG),
+                mybir.AxisListType.X,
+                ALU.add,
+            )
+
+        result = sbuf.tile([P, BAGS], F32)
+        nc.scalar.activation(result[:], bag_sums[:], GELU, bias=bias[:])
+        nc.sync.dma_start(out, result[:])

@@ -7,6 +7,7 @@ BAGS = N // BAG
 BLOCKS = K // P
 PIECE = 512
 PIECES = N // PIECE
+SQUARE = 32
 LIST_ROWS = 16
 
 FLOPS = 2 * K * M * N + 2 * M * N
@@ -26,15 +27,26 @@ def tile_rows_wbag_gelu_sub_kernel(tc, table, w, c, b, offs, out):
         weights = sbuf.tile([P, BLOCKS, M], BF16)
         offsets = sbuf.tile([P, N // LIST_ROWS], U16)
         bias = sbuf.tile([P, 1], F32)
-        entry_weights = sbuf.tile([P, N], F32)
+        c_rows = sbuf.tile([P, SQUARE], F32, align_bytes=64)
         words = [sbuf.tile([P, S], BF16, name=f"words{a}") for a in range(BLOCKS)]
 
         nc.sync.dma_start(offsets[:], offs)
+        c_square = c.rearrange("o (r q) -> o r q", q=SQUARE)
+        nc.scalar.dma_start(c_rows[:], c_square.to_broadcast([P // SQUARE, SQUARE, SQUARE]))
         nc.scalar.dma_start(weights[:], w.rearrange("(p a) m -> p a m", a=BLOCKS))
         for a in range(BLOCKS):
             nc.sync.dma_start(words[a][:], table_blocks[a])
-        nc.sync.dma_start(entry_weights[:], c[0].partition_broadcast(P))
         nc.scalar.dma_start(bias[:], b)
+
+        c_columns = sbuf.tile([P, SQUARE], F32, align_bytes=64)
+        c_repeated = sbuf.tile([P, N], F32, align_bytes=64)
+        entry_weights = sbuf.tile([P, N], F32, align_bytes=64)
+        nc.vector.transpose(c_columns[:], c_rows[:])
+        nc.vector.tensor_copy(
+            c_repeated[:].rearrange("p (r x) -> p r x", x=SQUARE),
+            c_columns[:].unsqueeze(2).to_broadcast([P, SQUARE, SQUARE]),
+        )
+        nc.vector.transpose(entry_weights[:], c_repeated[:])
 
         projected = [psum.tile([P, PIECE], F32, name=f"projected{i}") for i in range(PIECES)]
         columns = PIECE // LIST_ROWS

@@ -30,13 +30,14 @@ def tile_rows_wbag_gelu_sub_kernel(tc, table, w, c, b, offs, out):
         c_rows = sbuf.tile([P, SQUARE], F32, align_bytes=64)
         words = [sbuf.tile([P, S], BF16, name=f"words{a}") for a in range(BLOCKS)]
 
+        nc.scalar.dma_start(weights[:], w.rearrange("(p a) m -> p a m", a=BLOCKS))
+        nc.sync.dma_start(words[0][:], table_blocks[0])
         nc.sync.dma_start(offsets[:], offs)
         c_square = c.rearrange("o (r q) -> o r q", q=SQUARE)
-        nc.scalar.dma_start(c_rows[:], c_square.to_broadcast([P // SQUARE, SQUARE, SQUARE]))
-        nc.scalar.dma_start(weights[:], w.rearrange("(p a) m -> p a m", a=BLOCKS))
-        for a in range(BLOCKS):
+        nc.sync.dma_start(c_rows[:], c_square.to_broadcast([P // SQUARE, SQUARE, SQUARE]))
+        for a in range(1, BLOCKS):
             nc.sync.dma_start(words[a][:], table_blocks[a])
-        nc.scalar.dma_start(bias[:], b)
+        nc.sync.dma_start(bias[:], b)
 
         c_columns = sbuf.tile([P, SQUARE], F32, align_bytes=64)
         c_repeated = sbuf.tile([P, N], F32, align_bytes=64)

@@ -8,6 +8,10 @@ BLOCKS = K // P
 PIECE = 512
 PIECES = N // PIECE
 SQUARE = 32
+GROUPS = P // SQUARE
+CHUNK = 256
+CHUNKS = N // CHUNK
+ROW_STEP = SQUARE // CHUNKS
 LIST_ROWS = 16
 
 FLOPS = 2 * K * M * N + 2 * M * N
@@ -26,28 +30,34 @@ def tile_rows_wbag_gelu_sub_kernel(tc, table, w, c, b, offs, out):
         table_blocks = table.rearrange("(p a) s -> a p s", a=BLOCKS)
         weights = sbuf.tile([P, BLOCKS, M], BF16)
         offsets = sbuf.tile([P, N // LIST_ROWS], U16)
-        bias = sbuf.tile([P, 1], F32)
-        c_rows = sbuf.tile([P, SQUARE], F32, align_bytes=64)
+        c_rows = sbuf.tile([P, CHUNK], F32, align_bytes=64)
+        b_rows = sbuf.tile([P, SQUARE], F32, align_bytes=64)
         words = [sbuf.tile([P, S], BF16, name=f"words{a}") for a in range(BLOCKS)]
+
+        nc.vector.memset(c_rows[:], 0.0)
+        nc.vector.memset(b_rows[:], 0.0)
 
         nc.scalar.dma_start(weights[:], w.rearrange("(p a) m -> p a m", a=BLOCKS))
         nc.sync.dma_start(words[0][:], table_blocks[0])
         nc.sync.dma_start(offsets[:], offs)
-        c_square = c.rearrange("o (r q) -> o r q", q=SQUARE)
-        nc.sync.dma_start(c_rows[:], c_square.to_broadcast([P // SQUARE, SQUARE, SQUARE]))
+        c_chunks = c.rearrange("o (e y) -> o e y", y=CHUNK)
+        nc.sync.dma_start(c_rows[::ROW_STEP, :], c_chunks.to_broadcast([GROUPS, CHUNKS, CHUNK]))
+        nc.sync.dma_start(b_rows[::SQUARE, :], b.rearrange("(g q) o -> g (q o)", q=SQUARE))
         for a in range(1, BLOCKS):
             nc.sync.dma_start(words[a][:], table_blocks[a])
-        nc.sync.dma_start(bias[:], b)
 
-        c_columns = sbuf.tile([P, SQUARE], F32, align_bytes=64)
+        c_columns = sbuf.tile([P, CHUNK], F32, align_bytes=64)
         c_repeated = sbuf.tile([P, N], F32, align_bytes=64)
         entry_weights = sbuf.tile([P, N], F32, align_bytes=64)
         nc.vector.transpose(c_columns[:], c_rows[:])
+        c_values = c_columns[:, ::ROW_STEP].rearrange("p (s e) -> p e s", e=CHUNKS)
         nc.vector.tensor_copy(
-            c_repeated[:].rearrange("p (r x) -> p r x", x=SQUARE),
-            c_columns[:].unsqueeze(2).to_broadcast([P, SQUARE, SQUARE]),
+            c_repeated[:].rearrange("p (e s x) -> p e s x", e=CHUNKS, x=SQUARE),
+            c_values.unsqueeze(3).to_broadcast([P, CHUNKS, CHUNK // SQUARE, SQUARE]),
         )
         nc.vector.transpose(entry_weights[:], c_repeated[:])
+        b_columns = sbuf.tile([P, SQUARE], F32, align_bytes=64)
+        nc.vector.transpose(b_columns[:], b_rows[:])
 
         projected = [psum.tile([P, PIECE], F32, name=f"projected{i}") for i in range(PIECES)]
         columns = PIECE // LIST_ROWS
@@ -70,5 +80,5 @@ def tile_rows_wbag_gelu_sub_kernel(tc, table, w, c, b, offs, out):
             )
 
         result = sbuf.tile([P, BAGS], F32)
-        nc.scalar.activation(result[:], bag_sums[:], GELU, bias=bias[:])
+        nc.scalar.activation(result[:], bag_sums[:], GELU, bias=b_columns[:, 0:1])
         nc.sync.dma_start(out, result[:])

import concourse.mybir as mybir

P = 128
S, K, M, N = 2048, 512, 128, 1024
BAG = 16
BAGS = N // BAG
BLOCKS = K // P
PIECE = 512
PIECES = N // PIECE
SQUARE = 32
GROUPS = P // SQUARE
CHUNK = 256
CHUNKS = N // CHUNK
ROW_STEP = SQUARE // CHUNKS
LIST_ROWS = 16

FLOPS = 2 * K * M * N + 2 * M * N

BF16, F32, U16 = mybir.dt.bfloat16, mybir.dt.float32, mybir.dt.uint16
ALU = mybir.AluOpType
GELU = mybir.ActivationFunctionType.Gelu_apprx_tanh


def tile_rows_wbag_gelu_sub_kernel(tc, table, w, c, b, offs, out):
    nc = tc.nc
    with (
        tc.tile_pool(name="sbuf", bufs=1) as sbuf,
        tc.psum_pool(name="psum", bufs=1) as psum,
    ):
        table_blocks = table.rearrange("(p a) s -> a p s", a=BLOCKS)
        weights = sbuf.tile([P, BLOCKS, M], BF16)
        offsets = sbuf.tile([P, N // LIST_ROWS], U16)
        c_rows = sbuf.tile([P, CHUNK], F32, align_bytes=64)
        b_rows = sbuf.tile([P, SQUARE], F32, align_bytes=64)
        words = [sbuf.tile([P, S], BF16, name=f"words{a}") for a in range(BLOCKS)]

        nc.vector.memset(c_rows[:], 0.0)
        nc.vector.memset(b_rows[:], 0.0)

        nc.scalar.dma_start(weights[:], w.rearrange("(p a) m -> p a m", a=BLOCKS))
        nc.sync.dma_start(words[0][:], table_blocks[0])
        nc.sync.dma_start(offsets[:], offs)
        c_chunks = c.rearrange("o (e y) -> o e y", y=CHUNK)
        nc.sync.dma_start(c_rows[::ROW_STEP, :], c_chunks.to_broadcast([GROUPS, CHUNKS, CHUNK]))
        nc.sync.dma_start(b_rows[::SQUARE, :], b.rearrange("(g q) o -> g (q o)", q=SQUARE))
        for a in range(1, BLOCKS):
            nc.sync.dma_start(words[a][:], table_blocks[a])

        c_columns = sbuf.tile([P, CHUNK], F32, align_bytes=64)
        c_repeated = sbuf.tile([P, N], F32, align_bytes=64)
        entry_weights = sbuf.tile([P, N], F32, align_bytes=64)
        nc.vector.transpose(c_columns[:], c_rows[:])
        c_values = c_columns[:, ::ROW_STEP].rearrange("p (s e) -> p e s", e=CHUNKS)
        nc.vector.tensor_copy(
            c_repeated[:].rearrange("p (e s x) -> p e s x", e=CHUNKS, x=SQUARE),
            c_values.unsqueeze(3).to_broadcast([P, CHUNKS, CHUNK // SQUARE, SQUARE]),
        )
        nc.vector.transpose(entry_weights[:], c_repeated[:])
        b_columns = sbuf.tile([P, SQUARE], F32, align_bytes=64)
        nc.vector.transpose(b_columns[:], b_rows[:])

        projected = [psum.tile([P, PIECE], F32, name=f"projected{i}") for i in range(PIECES)]
        columns = PIECE // LIST_ROWS
        for a in range(BLOCKS):
            for i in range(PIECES):
                picked = words[a][:].indirect(offsets[:, i * columns : (i + 1) * columns])
                nc.tensor.matmul(projected[i][:], weights[:, a, :], picked, start=a == 0, stop=a == BLOCKS - 1)

        weighted = sbuf.tile([P, N], F32)
        bag_sums = sbuf.tile([P, BAGS], F32)
        for i in range(PIECES):
            entries = slice(i * PIECE, (i + 1) * PIECE)
            bags = slice(i * PIECE // BAG, (i + 1) * PIECE // BAG)
            nc.vector.tensor_tensor(weighted[:, entries], projected[i][:], entry_weights[:, entries], ALU.mult)
            nc.vector.tensor_reduce(
                bag_sums[:, bags],
                weighted[:, entries].rearrange("p (v t) -> p v t", t=BAG),
                mybir.AxisListType.X,
                ALU.add,
            )

        result = sbuf.tile([P, BAGS], F32)
        nc.scalar.activation(result[:], bag_sums[:], GELU, bias=b_columns[:, 0:1])
        nc.sync.dma_start(out, result[:])
